import numpy as np
CORES = [2,10,18,26,34,42,50,58,66,74,82,90,98,106,114,122,130,138,146,154,162,170,178,186,194,202,210,218,226,234,242,250,258,266,274,282,290,298,306,314,322,330,338,346,354,362,370,378,386,394,402,410,418,426,434,442,450,458,466,474,482,490,498,506]
N = 64
TOK, D = 24, 1024
ROUTE = [[[47,48],[15,39],[11,38],[57,60],[13,34],[11,14],[28,57],[28,43],[36,47],[2,8],[2,48],[17,37],[22,53],[0,10],[19,61],[6,37],[29,61],[24,25],[17,38],[15,29],[5,28],[16,42],[16,61],[46,61]],[[33,45],[7,19],[14,60],[10,54],[7,43],[36,52],[8,43],[16,49],[3,43],[9,34],[36,44],[26,41],[30,34],[9,59],[37,54],[23,62],[30,60],[12,16],[38,50],[18,51],[41,63],[25,47],[32,42],[11,14]],[[55,62],[20,49],[9,18],[14,15],[12,21],[5,56],[29,33],[12,46],[12,40],[44,58],[10,26],[37,55],[1,38],[12,27],[13,20],[43,57],[9,61],[7,46],[8,27],[15,39],[15,26],[2,20],[6,35],[0,26]],[[5,42],[11,15],[41,52],[1,11],[29,43],[10,46],[28,38],[50,62],[19,45],[28,57],[0,43],[30,42],[7,48],[13,55],[12,20],[14,28],[17,32],[9,50],[10,61],[21,42],[40,57],[3,52],[38,46],[3,59]],[[35,39],[16,38],[0,43],[17,54],[48,53],[0,1],[12,48],[47,62],[7,59],[1,27],[1,57],[19,21],[17,26],[1,35],[6,54],[36,51],[19,25],[30,61],[37,49],[56,62],[5,27],[22,30],[41,63],[21,60]],[[44,46],[17,23],[12,51],[13,49],[56,59],[34,53],[1,24],[15,25],[27,50],[40,43],[4,46],[14,32],[12,60],[18,33],[34,56],[54,58],[9,56],[21,48],[33,38],[5,53],[0,52],[39,53],[18,27],[20,54]],[[12,20],[36,48],[51,52],[6,10],[15,62],[50,52],[14,42],[9,33],[35,45],[22,60],[6,46],[17,33],[1,27],[17,26],[15,49],[51,58],[46,54],[27,54],[1,52],[6,46],[5,48],[49,53],[3,56],[8,20]],[[27,56],[7,32],[50,54],[39,46],[6,20],[48,60],[44,60],[33,40],[11,16],[10,38],[6,13],[11,22],[3,4],[11,19],[5,63],[35,53],[6,52],[26,42],[16,61],[23,58],[11,63],[0,40],[45,47],[11,36]],[[3,17],[45,53],[0,3],[35,37],[22,31],[27,30],[46,63],[14,58],[37,47],[20,62],[22,37],[38,48],[14,42],[3,58],[53,61],[43,63],[24,42],[38,61],[15,62],[44,50],[22,23],[27,54],[40,61],[19,30]],[[52,62],[21,26],[38,54],[13,26],[0,5],[8,14],[49,63],[8,28],[7,17],[22,25],[14,42],[57,58],[18,52],[9,31],[45,57],[28,29],[18,41],[5,42],[22,35],[27,35],[23,40],[28,55],[8,58],[1,49]],[[3,45],[1,37],[0,21],[36,48],[26,49],[55,57],[4,55],[5,19],[25,41],[31,46],[22,62],[13,44],[27,34],[41,62],[43,61],[1,32],[29,36],[42,58],[17,63],[37,54],[14,24],[9,19],[2,49],[3,46]],[[26,34],[19,45],[38,42],[23,63],[13,29],[14,31],[26,58],[39,40],[51,59],[57,59],[12,61],[0,21],[13,16],[19,59],[8,23],[44,46],[29,63],[25,49],[4,44],[29,42],[26,45],[20,63],[33,61],[16,36]],[[9,17],[6,38],[45,53],[15,39],[53,54],[10,34],[27,42],[3,22],[38,54],[23,62],[34,50],[19,47],[18,24],[47,61],[39,49],[14,15],[4,19],[8,11],[3,17],[9,13],[59,63],[14,40],[27,40],[33,46]],[[14,42],[26,53],[19,23],[5,37],[0,14],[35,41],[22,35],[7,38],[59,62],[23,51],[35,51],[36,49],[29,50],[0,48],[18,41],[32,61],[37,48],[23,44],[35,37],[12,60],[16,44],[17,57],[10,12],[20,49]],[[7,61],[17,33],[40,56],[51,54],[28,40],[48,53],[7,53],[58,63],[41,52],[2,38],[4,47],[6,46],[10,54],[59,61],[31,38],[17,24],[1,47],[16,18],[37,62],[17,48],[24,52],[31,37],[34,41],[1,8]],[[10,45],[35,40],[17,26],[3,36],[46,48],[9,47],[2,15],[56,57],[9,17],[10,13],[38,44],[35,43],[28,50],[53,59],[23,26],[4,13],[18,22],[27,39],[7,45],[27,55],[43,62],[6,58],[25,42],[7,9]],[[57,61],[21,38],[10,12],[6,59],[23,60],[19,27],[11,15],[36,46],[48,53],[18,51],[33,50],[16,21],[6,58],[2,4],[20,59],[35,62],[0,49],[18,62],[9,41],[38,59],[2,44],[30,37],[33,57],[1,18]],[[24,55],[7,21],[6,21],[12,56],[17,18],[62,63],[24,27],[47,52],[17,23],[5,35],[40,58],[29,60],[28,63],[31,40],[8,30],[10,37],[23,28],[14,36],[38,63],[2,56],[21,29],[29,30],[12,63],[19,61]],[[3,42],[20,60],[0,54],[2,61],[23,27],[20,41],[0,50],[3,20],[6,39],[42,52],[30,35],[35,40],[18,42],[48,63],[17,61],[6,42],[4,18],[20,61],[54,60],[14,29],[32,40],[7,63],[23,53],[20,48]],[[48,54],[23,27],[38,53],[62,63],[16,53],[37,44],[35,45],[31,60],[19,44],[7,42],[24,36],[34,56],[48,51],[0,18],[21,54],[29,51],[56,61],[10,26],[20,30],[3,52],[16,43],[24,26],[34,41],[7,41]],[[17,38],[4,26],[46,50],[21,47],[21,60],[36,46],[53,60],[34,52],[24,55],[43,56],[50,59],[8,37],[10,55],[20,61],[13,19],[2,4],[34,58],[11,49],[58,59],[24,42],[4,34],[43,60],[11,22],[12,24]],[[15,49],[33,50],[40,61],[29,60],[18,23],[48,53],[14,43],[39,47],[42,44],[17,40],[18,41],[20,27],[17,38],[58,62],[1,52],[42,45],[24,58],[21,28],[43,59],[40,52],[2,14],[2,50],[29,59],[11,58]],[[22,40],[16,40],[3,32],[10,62],[16,19],[4,18],[7,45],[26,33],[15,32],[11,50],[8,13],[45,63],[9,22],[27,52],[2,10],[42,50],[2,31],[45,48],[3,42],[4,49],[30,63],[34,53],[3,45],[12,63]],[[10,28],[3,62],[16,26],[42,54],[23,55],[18,59],[51,57],[59,62],[10,57],[8,36],[29,39],[7,43],[31,44],[12,57],[33,63],[44,51],[32,55],[20,25],[57,61],[25,58],[23,36],[20,39],[54,58],[19,28]],[[17,63],[17,46],[0,27],[8,21],[5,15],[53,56],[16,59],[30,53],[31,34],[48,53],[8,40],[0,55],[31,62],[26,56],[37,58],[24,45],[30,46],[16,62],[17,21],[12,62],[15,20],[25,41],[57,63],[27,57]],[[0,63],[52,62],[3,56],[50,61],[6,13],[26,34],[13,43],[28,57],[42,53],[37,57],[29,32],[9,59],[25,37],[12,49],[17,61],[34,51],[35,47],[26,40],[28,47],[3,32],[38,42],[11,48],[37,57],[13,40]],[[10,40],[19,41],[6,41],[26,58],[5,14],[3,25],[11,19],[22,51],[16,32],[5,42],[42,58],[56,60],[31,35],[0,30],[8,38],[3,50],[8,34],[37,59],[11,58],[19,24],[25,63],[2,41],[4,57],[1,2]],[[26,42],[10,38],[21,38],[5,53],[26,36],[37,42],[31,38],[1,39],[50,58],[17,49],[21,49],[40,51],[53,58],[6,41],[3,23],[33,36],[6,52],[11,56],[18,43],[17,55],[16,32],[15,63],[21,51],[30,49]],[[26,37],[14,26],[43,63],[6,13],[40,42],[1,62],[15,61],[17,53],[37,41],[56,62],[15,38],[39,52],[11,13],[5,53],[39,43],[8,24],[1,2],[50,63],[7,61],[23,29],[4,6],[35,57],[7,33],[12,49]],[[14,48],[15,45],[7,23],[14,21],[11,45],[18,20],[27,41],[40,44],[28,35],[35,50],[37,41],[32,45],[17,57],[42,57],[25,45],[46,55],[2,49],[31,34],[40,63],[29,57],[25,32],[25,49],[4,51],[1,55]],[[7,33],[1,6],[39,47],[45,51],[4,13],[20,42],[10,37],[6,54],[14,59],[49,61],[8,10],[14,20],[13,41],[41,62],[12,62],[5,42],[58,61],[20,41],[22,57],[4,7],[41,62],[28,63],[28,51],[11,50]],[[9,39],[17,52],[25,61],[45,59],[18,29],[41,49],[19,44],[50,60],[16,34],[28,34],[27,54],[22,50],[15,17],[3,51],[16,42],[29,44],[8,26],[5,25],[32,62],[14,53],[6,55],[21,57],[21,62],[40,50]],[[2,27],[33,56],[11,47],[5,34],[24,60],[5,24],[23,35],[0,45],[40,51],[49,60],[33,47],[5,25],[44,47],[22,60],[0,35],[20,46],[1,21],[4,26],[18,30],[33,35],[2,43],[3,52],[34,35],[1,21]],[[38,49],[13,51],[29,48],[23,42],[0,25],[19,54],[24,34],[42,45],[4,37],[3,30],[38,53],[43,48],[60,61],[0,2],[3,19],[21,57],[18,19],[8,34],[8,14],[16,42],[0,44],[41,48],[27,38],[26,57]],[[8,39],[33,62],[24,59],[28,57],[11,21],[0,47],[9,35],[13,15],[36,39],[18,23],[22,36],[12,26],[13,40],[5,6],[36,51],[22,26],[27,48],[35,51],[6,18],[11,36],[38,47],[34,42],[19,34],[22,28]],[[37,39],[21,38],[12,43],[51,55],[42,50],[24,47],[24,40],[36,45],[40,54],[52,60],[17,29],[24,56],[57,61],[3,58],[12,53],[4,35],[43,45],[17,38],[3,10],[38,43],[13,14],[1,32],[30,52],[18,28]],[[3,7],[4,21],[16,35],[60,62],[28,56],[7,27],[15,62],[9,28],[19,60],[25,54],[13,58],[36,46],[2,27],[0,56],[7,32],[44,53],[56,60],[35,42],[1,53],[9,61],[8,48],[17,31],[32,54],[12,34]],[[37,49],[35,42],[1,41],[34,35],[3,21],[46,55],[32,57],[28,49],[2,8],[15,48],[23,60],[4,28],[18,40],[20,43],[12,49],[11,34],[12,47],[20,39],[11,37],[32,49],[3,15],[26,55],[2,29],[15,42]],[[8,37],[2,53],[12,16],[27,40],[29,53],[0,45],[15,43],[15,40],[0,30],[34,61],[34,45],[21,50],[10,33],[36,49],[24,39],[5,59],[7,41],[42,49],[40,49],[17,53],[15,58],[38,55],[13,17],[20,41]],[[21,57],[16,39],[9,34],[32,58],[11,55],[12,60],[15,16],[47,49],[49,54],[49,51],[7,30],[46,62],[56,59],[10,42],[27,39],[28,51],[8,45],[10,56],[7,15],[17,55],[40,46],[20,41],[22,57],[37,54]],[[8,16],[15,25],[33,59],[27,30],[19,22],[43,61],[13,57],[10,49],[32,50],[28,54],[26,59],[47,62],[6,49],[14,21],[2,54],[32,45],[37,46],[10,28],[48,53],[0,4],[17,59],[6,33],[2,24],[49,56]],[[38,55],[0,52],[7,50],[20,38],[9,22],[11,42],[8,15],[19,58],[9,53],[48,63],[33,38],[4,37],[18,24],[8,53],[1,46],[5,21],[10,53],[34,45],[26,52],[3,24],[22,30],[11,32],[4,58],[44,58]],[[13,33],[8,25],[53,62],[50,54],[18,32],[24,29],[3,11],[17,33],[14,20],[30,37],[23,57],[14,58],[24,56],[8,23],[30,45],[28,30],[17,60],[20,49],[6,52],[24,37],[2,44],[1,49],[5,14],[48,54]],[[23,35],[19,45],[8,31],[4,37],[17,30],[16,63],[26,38],[42,58],[10,46],[16,34],[19,40],[27,33],[20,44],[35,54],[21,35],[44,55],[20,52],[9,49],[19,28],[42,60],[44,57],[23,42],[16,63],[2,55]],[[19,20],[18,21],[48,50],[11,23],[4,6],[12,59],[2,22],[50,60],[12,26],[27,38],[61,62],[41,58],[18,34],[29,40],[35,42],[16,46],[39,45],[0,48],[47,49],[9,32],[3,35],[40,62],[3,49],[32,57]],[[28,60],[5,10],[18,57],[9,20],[6,32],[9,23],[26,44],[5,14],[7,45],[18,24],[36,48],[49,52],[23,60],[16,33],[21,22],[12,56],[22,62],[2,61],[20,22],[9,15],[1,39],[34,58],[40,59],[35,45]],[[40,46],[4,7],[14,20],[4,35],[53,55],[41,52],[16,37],[43,52],[17,28],[57,59],[26,47],[3,12],[12,55],[14,50],[18,22],[50,55],[1,60],[10,11],[47,54],[0,20],[52,58],[7,28],[27,37],[1,50]],[[7,24],[0,3],[10,59],[7,20],[26,41],[3,53],[36,47],[5,51],[7,40],[4,38],[41,61],[16,55],[8,35],[8,40],[18,57],[49,59],[51,60],[2,6],[5,48],[22,47],[11,12],[34,55],[0,18],[43,56]],[[4,10],[41,63],[4,30],[20,29],[6,26],[24,61],[40,41],[15,45],[20,23],[34,39],[20,52],[7,20],[15,46],[37,56],[9,45],[23,38],[8,9],[30,39],[37,59],[34,47],[23,29],[43,52],[33,35],[42,63]],[[5,60],[30,61],[24,31],[13,16],[5,54],[25,40],[6,18],[56,58],[11,24],[3,49],[16,40],[6,62],[13,29],[21,51],[53,60],[13,27],[47,55],[33,56],[25,55],[40,44],[9,30],[26,51],[6,43],[51,62]],[[45,54],[16,57],[43,63],[33,53],[27,49],[12,27],[9,47],[13,55],[15,26],[18,60],[15,27],[45,60],[26,29],[50,61],[3,6],[42,46],[40,51],[8,48],[23,49],[0,53],[23,47],[10,51],[15,62],[6,38]],[[29,40],[4,63],[38,50],[21,28],[6,40],[48,52],[30,32],[15,45],[38,58],[39,48],[7,63],[5,59],[43,48],[13,38],[16,54],[20,61],[37,54],[55,57],[5,31],[33,35],[5,43],[13,24],[2,47],[18,21]],[[12,48],[14,63],[25,44],[22,63],[14,17],[16,50],[4,22],[13,40],[14,45],[26,45],[12,33],[0,31],[7,52],[43,48],[32,58],[9,35],[41,61],[7,49],[33,51],[19,21],[2,33],[58,61],[10,16],[28,59]],[[3,63],[11,13],[55,57],[12,60],[46,57],[14,41],[23,29],[12,52],[14,35],[18,21],[31,38],[8,53],[1,8],[5,60],[5,33],[18,55],[25,39],[1,62],[2,24],[10,34],[7,24],[44,45],[34,61],[22,47]],[[28,60],[25,43],[19,40],[35,55],[44,47],[45,49],[10,43],[51,54],[13,59],[11,48],[38,59],[38,54],[12,49],[47,56],[24,54],[21,52],[33,55],[10,38],[48,51],[8,32],[5,11],[40,58],[32,56],[45,63]],[[24,42],[46,63],[16,21],[39,59],[7,17],[35,63],[13,45],[38,51],[35,42],[28,48],[28,32],[7,9],[5,35],[25,31],[21,44],[13,36],[26,43],[14,22],[2,55],[14,37],[40,49],[31,62],[7,62],[27,56]],[[9,41],[1,42],[13,20],[28,62],[19,25],[21,35],[26,63],[41,62],[2,54],[32,47],[18,53],[7,60],[0,34],[23,50],[32,48],[0,21],[39,61],[28,29],[2,11],[6,54],[5,27],[8,31],[9,59],[12,33]],[[15,42],[7,56],[7,39],[11,42],[26,53],[18,27],[22,55],[8,59],[8,42],[1,29],[3,6],[14,26],[24,28],[22,52],[51,60],[55,57],[47,50],[27,33],[24,33],[35,42],[11,29],[19,20],[28,58],[25,34]],[[20,38],[15,49],[31,55],[8,11],[12,47],[10,33],[61,62],[11,48],[16,35],[16,36],[20,26],[36,44],[3,30],[32,58],[14,40],[30,34],[15,47],[32,45],[32,49],[47,56],[6,17],[9,39],[43,59],[19,40]],[[9,58],[9,27],[23,63],[35,43],[12,25],[7,46],[27,51],[6,33],[0,49],[41,58],[35,50],[27,47],[6,8],[2,51],[33,53],[30,31],[2,45],[59,62],[57,63],[55,59],[42,61],[52,62],[15,40],[5,35]],[[34,61],[33,54],[42,47],[16,17],[45,48],[46,58],[0,43],[9,13],[26,40],[45,61],[29,47],[5,33],[47,61],[15,39],[5,41],[26,31],[17,57],[57,58],[29,63],[61,62],[1,13],[46,60],[3,57],[24,31]],[[26,50],[5,28],[17,29],[40,62],[1,10],[51,53],[33,55],[19,31],[0,34],[14,41],[31,44],[13,38],[1,29],[45,49],[19,43],[20,58],[8,22],[29,58],[21,63],[2,11],[20,40],[22,52],[4,22],[34,39]],[[11,57],[12,42],[15,51],[5,39],[10,53],[22,31],[0,57],[10,24],[8,35],[8,26],[32,43],[10,59],[39,59],[51,58],[27,37],[41,49],[25,51],[13,24],[10,43],[21,45],[52,60],[28,46],[17,43],[51,63]],[[26,27],[26,63],[10,59],[39,54],[10,15],[10,12],[46,54],[5,42],[11,14],[26,39],[36,43],[24,45],[25,57],[2,3],[33,54],[56,58],[5,34],[13,18],[12,40],[33,44],[34,62],[16,32],[5,39],[20,44]]]
CAP = 48
def setup_inputs(rng):
    return {"z": rng.standard_normal((N, CAP, D), dtype=np.float32), "x": rng.standard_normal((N, TOK, D), dtype=np.float32)}
def reference(z, x):
    y = x.astype(np.float64)
    fill = [0] * N
    for r in range(N):
        for t in range(TOK):
            for e in ROUTE[r][t]:
                if fill[e] < CAP:
                    y[r][t] += z[e][fill[e]]
                    fill[e] += 1
    return {"y": y.astype(z.dtype)}

@@ -1,0 +1,362 @@
+from concourse.bass import DstId, RemoteDMATransfer
+from concourse.mybir import AluOpType
+import comms_topo as ct
+
+SCRATCH = {
+    "rows": ("dram", [48, 128, 8], "float32"),
+    "land": ("dram", [24, 128, 8], "float32"),
+}
+SEMAPHORES = ["loaded", "read", "s1", "s2", "fin", "stored"]
+
+CACHE = {}
+
+SCALE = {"co": 48, "ci": 24, "po": 50, "pi": 50, "mate": 14, "so": 26, "si": 26, "cable": 8}
+POWER = 8
+PASSES = 4
+
+
+def kept_results(route, cap):
+    n = len(route)
+    fill = [0] * n
+    res = {}
+    for r in range(n):
+        for t in range(len(route[r])):
+            got = []
+            for e in route[r][t]:
+                if fill[e] < cap:
+                    got.append((e, fill[e]))
+                    fill[e] += 1
+            res[(r, t)] = got
+    return res, fill
+
+
+def links(src, dst):
+    out = [("co", src), ("ci", dst)]
+    hs, hd = ct.host(src), ct.host(dst)
+    cs, cd = ct.chip(src), ct.chip(dst)
+    if (hs, cs) == (hd, cd):
+        return out
+    out += [("po", hs, cs), ("pi", hd, cd)]
+    die = (src % 8) // 4
+    if ct.rack(hs) == ct.rack(hd):
+        c = cs
+        if (cs ^ cd) & 1:
+            out.append(("mate", hs, cs, die))
+            c = cs ^ 1
+        if (hs, c) != (hd, cd):
+            out += [("so", hs, c, die), ("si", hd, cd, die)]
+    elif cs == cd:
+        out.append(("cable", hs, cs, (src % 8) // 2))
+    return out
+
+
+def tree_writes(node, parent, cores, acc):
+    if node[0] == "z":
+        acc.append((cores[node[1]], parent))
+    else:
+        acc.append((node[1], parent))
+        for ch in node[2]:
+            tree_writes(ch, node[1], cores, acc)
+
+
+def candidates(r, ext, cores, group):
+    rc = cores[r]
+    H = ct.host(rc)
+    D, P, C = H ^ 2, H ^ 1, 3 - H
+
+    def helpers(h, c, dst):
+        base = h * 128 + c * 8
+        return [k for k in range(base, base + 8) if k not in group and k != dst and ct.may_write(k, dst)]
+
+    def hc(core):
+        return ct.host(core), ct.chip(core)
+
+    out = []
+    if not ext:
+        return [(None, None)]
+    leaves = [("z", e, j) for e, j in ext]
+    ec = [cores[e] for e, j in ext]
+    eh = [ct.host(c) for c in ec]
+    if len(ext) == 1:
+        if eh[0] != D:
+            return [(None, leaves[0])]
+        for R in helpers(C, ct.chip(rc), rc):
+            out.append(("C", ("n", R, (leaves[0],))))
+        for R in helpers(P, ct.chip(ec[0]), rc):
+            out.append(("P", ("n", R, (leaves[0],))))
+        return out
+    nD = eh.count(D)
+    if nD == 0:
+        if eh[0] == eh[1]:
+            chips = [hc(ec[0]), hc(ec[1])] + ([hc(rc)] if eh[0] == H else [])
+        elif H in eh:
+            chips = [hc(ec[eh.index(H)]), hc(rc)]
+        else:
+            chips = [hc(rc)]
+        for h, c in chips:
+            for F in helpers(h, c, rc):
+                out.append((None, ("n", F, tuple(leaves))))
+        return out
+    if nD == 1:
+        i = eh.index(D)
+        o = 1 - i
+        if eh[o] != H:
+            h, c = hc(ec[o])
+            for F in helpers(h, c, rc):
+                out.append((None, ("n", F, tuple(leaves))))
+            return out
+        for h, c in (hc(ec[o]), hc(rc)):
+            for F in helpers(h, c, rc):
+                for R in helpers(C, c, F):
+                    out.append(("C", ("n", F, (leaves[o], ("n", R, (leaves[i],))))))
+                for R in helpers(P, ct.chip(ec[i]), F):
+                    out.append(("P", ("n", F, (leaves[o], ("n", R, (leaves[i],))))))
+        return out
+    for i in (0, 1):
+        h, c = hc(ec[i])
+        for R in helpers(C, ct.chip(rc), rc):
+            for F in helpers(h, c, R):
+                out.append(("C", ("n", R, (("n", F, tuple(leaves)),))))
+        for R in helpers(P, c, rc):
+            for F in helpers(h, c, R):
+                out.append(("P", ("n", R, (("n", F, tuple(leaves)),))))
+    return out
+
+
+def split_flexible(cand, cores):
+    hin, hout = [0] * 4, [0] * 4
+    pair = {}
+    flex = [0] * 4
+    for (r, t), cl in cand.items():
+        via, tree = cl[0][0], cl[0][1]
+        H = ct.host(cores[r])
+        if tree is None:
+            continue
+        if via is not None:
+            flex[H] += 1
+            hout[H ^ 2] += 1
+            hin[H] += 1
+            continue
+        acc = []
+        tree_writes(tree, cores[r], cores, acc)
+        for s, d in acc:
+            hs, hd = ct.host(s), ct.host(d)
+            if hs != hd:
+                hout[hs] += 1
+                hin[hd] += 1
+                if ct.rack(hs) != ct.rack(hd):
+                    pair[(hs, hd)] = pair.get((hs, hd), 0) + 1
+    per_rack = []
+    for a in (0, 2):
+        b = a + 1
+        opts = []
+        for xa in range(flex[a] + 1):
+            for xb in range(flex[b] + 1):
+                pa = pair.get((3 - a, a), 0) + xa + flex[b] - xb
+                pb = pair.get((3 - b, b), 0) + xb + flex[a] - xa
+                opts.append((max(pa, pb), xa, xb))
+        least = min(opts)[0]
+        per_rack.append([(xa, xb) for m, xa, xb in opts if m == least])
+    best = None
+    for x0, x1 in per_rack[0]:
+        for x2, x3 in per_rack[1]:
+            x = (x0, x1, x2, x3)
+            relay = [0] * 4
+            for H in range(4):
+                relay[3 - H] += x[H]
+                relay[H ^ 1] += flex[H] - x[H]
+            mi = max(hin[h] + relay[h] for h in range(4))
+            mo = max(hout[h] + relay[h] for h in range(4))
+            key = (max(mi, mo), mi + mo, x)
+            if best is None or key < best:
+                best = key
+    return best[2]
+
+
+def choose_routes(route, cap, cores):
+    group = set(cores)
+    res, fill = kept_results(route, cap)
+    lcache = {}
+    cand = {}
+    for (r, t), got in res.items():
+        ext = [(e, j) for e, j in got if e != r]
+        cl = []
+        for via, tree in candidates(r, ext, cores, group):
+            acc = []
+            if tree is not None:
+                tree_writes(tree, cores[r], cores, acc)
+            rs = []
+            for sd in acc:
+                if sd not in lcache:
+                    lcache[sd] = links(sd[0], sd[1])
+                rs += lcache[sd]
+            cl.append((via, tree, rs))
+        cand[(r, t)] = cl
+    quota = split_flexible(cand, cores)
+    tab = {c: [(i / s) ** POWER for i in range(600)] for c, s in SCALE.items()}
+    load = {}
+
+    def delta(rs):
+        d = 0.0
+        seen = {}
+        for k in rs:
+            n = load.get(k, 0) + seen.get(k, 0)
+            tb = tab[k[0]]
+            d += tb[n + 1] - tb[n]
+            seen[k] = seen.get(k, 0) + 1
+        return d
+
+    def add(rs, s):
+        for k in rs:
+            load[k] = load.get(k, 0) + s
+
+    def best(key, via):
+        cl = cand[key]
+        bi, bd = None, None
+        for i in range(len(cl)):
+            if cl[i][0] == via:
+                d = delta(cl[i][2])
+                if bd is None or d < bd:
+                    bi, bd = i, d
+        return bi, bd
+
+    choice, way = {}, {}
+    keys = sorted(cand)
+    for k in keys:
+        if cand[k][0][0] is None:
+            way[k] = None
+            choice[k] = best(k, None)[0]
+            add(cand[k][choice[k]][2], 1)
+    for H in range(4):
+        diffs = sorted((best(k, "C")[1] - best(k, "P")[1], k)
+                       for k in keys if cand[k][0][0] is not None and ct.host(cores[k[0]]) == H)
+        for n in range(len(diffs)):
+            way[diffs[n][1]] = "C" if n < quota[H] else "P"
+    for k in keys:
+        if way[k] is not None:
+            choice[k] = best(k, way[k])[0]
+            add(cand[k][choice[k]][2], 1)
+    for p in range(PASSES):
+        for k in keys:
+            if len(cand[k]) > 1:
+                add(cand[k][choice[k]][2], -1)
+                choice[k] = best(k, way[k])[0]
+                add(cand[k][choice[k]][2], 1)
+    return res, fill, {k: cand[k][choice[k]][1] for k in keys}
+
+
+def build_plan(route, cap, cores):
+    res, fill, trees = choose_routes(route, cap, cores)
+    sends = {}
+    expect = {}
+    used = {}
+
+    def emit(core, phase, srcs, dst, buf, slot, sem):
+        sends.setdefault(core, {}).setdefault(phase, []).append((srcs, dst, buf, slot, sem))
+        ex = expect.setdefault(dst, {})
+        ex[sem] = ex.get(sem, 0) + 1
+
+    def walk(node, dst, buf, slot, final):
+        if node[0] == "z":
+            emit(cores[node[1]], 0, [node[2]], dst, buf, slot, "fin" if final else "s1")
+            return 0
+        me = node[1]
+        slots, phase = [], 0
+        for ch in node[2]:
+            s = used.get(me, 0)
+            used[me] = s + 1
+            slots.append(s)
+            phase = max(phase, walk(ch, me, "rows", s, False))
+        phase += 1
+        emit(me, phase, slots, dst, buf, slot, "fin" if final else "s%d" % (phase + 1))
+        return phase
+
+    for (r, t) in sorted(trees):
+        if trees[(r, t)] is not None:
+            walk(trees[(r, t)], cores[r], "land", t, True)
+    own, landed = {}, {}
+    for (r, t), got in sorted(res.items()):
+        for e, j in got:
+            if e == r:
+                own.setdefault(r, []).append((t, j))
+        if trees[(r, t)] is not None:
+            landed.setdefault(r, []).append(t)
+    return {"sends": sends, "expect": expect, "fill": fill, "own": own, "landed": landed}
+
+
+def issue(g, core, T, batch):
+    sem = {"s1": T.sem.s1, "s2": T.sem.s2, "fin": T.sem.fin}
+    buf = {"rows": T.rows, "land": T.land}
+    far = [s for s in batch if ct.mask(core, s[1]) != 0xFFFF]
+    near = [s for s in batch if ct.mask(core, s[1]) == 0xFFFF]
+    while far or near:
+        bits = list(range(16))
+        now = []
+        for s in far[:8]:
+            now.append((s, bits.pop(0)))
+        far = far[8:]
+        take = near[:len(bits)]
+        near = near[len(bits):]
+        for s in take:
+            now.append((s, bits.pop()))
+        transfers = []
+        for (srcs, dst, b, slot, sm), bit in now:
+            rid, pid = ct.addr(dst, core)
+            if len(srcs) == 1:
+                transfers.append(RemoteDMATransfer(dst_ids=[DstId(rid=rid, pnc=pid)], dma_engine_mask=1 << bit,
+                                                   remote_sem=sem[sm], src=T.rows[srcs[0]], dst=buf[b][slot]))
+            else:
+                transfers.append(RemoteDMATransfer(dst_ids=[DstId(rid=rid, pnc=pid)], dma_engine_mask=1 << bit,
+                                                   remote_sem=sem[sm], srcs=[T.rows[s] for s in srcs],
+                                                   dsts=[buf[b][slot]], alu_op=1))
+        g.remote_dma_fused(transfers, local_sem=T.sem.read)
+    return len(batch)
+
+
+def runs_of(tokens):
+    out = []
+    for t in tokens:
+        if out and out[-1][1] == t:
+            out[-1][1] = t + 1
+        else:
+            out.append([t, t + 1])
+    return out
+
+
+def rank_program(g, core, T, topo):
+    if "plan" not in CACHE:
+        CACHE["plan"] = build_plan(T.tables["ROUTE"], T.tables["CAP"], list(T.cores))
+    plan = CACHE["plan"]
+    sends = plan["sends"].get(core, {})
+    expect = plan["expect"].get(core, {})
+    rank = T.rank_of(core)
+    if rank is None:
+        sent = 0
+        for phase, sm in ((1, T.sem.s1), (2, T.sem.s2)):
+            n = expect.get("s%d" % phase, 0)
+            if n:
+                g.wait_ge(sm, n)
+            if sends.get(phase):
+                sent += issue(g, core, T, sends[phase])
+        if sent:
+            g.wait_ge(T.sem.read, sent)
+        return
+    n = plan["fill"][rank]
+    stored = 16
+    g.dma_start(T.rows[0:n], T.z[0:n]).then_inc(T.sem.loaded, 16)
+    g.dma_start(T.y[:], T.x[:]).then_inc(T.sem.stored, 16)
+    g.wait_ge(T.sem.loaded, 16)
+    sent = issue(g, core, T, sends.get(0, []))
+    g.wait_ge(T.sem.stored, stored)
+    for t, j in plan["own"].get(rank, []):
+        g.dma_start(T.y[t:t + 1], T.z[j:j + 1], accum_op=AluOpType.add).then_inc(T.sem.stored, 16)
+        stored += 16
+    g.wait_ge(T.sem.stored, stored)
+    if expect.get("fin", 0):
+        g.wait_ge(T.sem.fin, expect["fin"])
+    for a, b in runs_of(plan["landed"].get(rank, [])):
+        g.dma_start(T.y[a:b], T.land[a:b], accum_op=AluOpType.add, max_dma_last_dim=4096).then_inc(T.sem.stored, 16)
+        stored += 16
+    g.wait_ge(T.sem.stored, stored)
+    if sent:
+        g.wait_ge(T.sem.read, sent)

@@ -10,9 +10,13 @@ SEMAPHORES = ["loaded", "read", "s1", "s2", "fin", "stored"]
 
 CACHE = {}
 
-SCALE = {"co": 48, "ci": 24, "po": 50, "pi": 50, "mate": 14, "so": 26, "si": 26, "cable": 8}
-POWER = 8
-PASSES = 4
+OUTBOUND = (1, 5, 7)
+INBOUND = (0, 3, 4, 6)
+EITHER = (0, 1, 3, 4, 5, 6, 7)
+
+SCALE = {"co": 48, "ci": 24, "po": 48, "pi": 48, "mate": 12, "so": 20, "si": 20, "cable": 4, "off": 32}
+POWER = 12
+PASSES = 6
 
 
 def kept_results(route, cap):
@@ -30,13 +34,15 @@ def kept_results(route, cap):
     return res, fill
 
 
-def links(src, dst):
+def links(src, dst, group):
     out = [("co", src), ("ci", dst)]
     hs, hd = ct.host(src), ct.host(dst)
     cs, cd = ct.chip(src), ct.chip(dst)
     if (hs, cs) == (hd, cd):
         return out
     out += [("po", hs, cs), ("pi", hd, cd)]
+    if src in group:
+        out.append(("off", src))
     die = (src % 8) // 4
     if ct.rack(hs) == ct.rack(hd):
         c = cs
@@ -59,42 +65,53 @@ def tree_writes(node, parent, cores, acc):
             tree_writes(ch, node[1], cores, acc)
 
 
-def candidates(r, ext, cores, group):
+def candidates(r, got, cores, group):
     rc = cores[r]
     H = ct.host(rc)
     D, P, C = H ^ 2, H ^ 1, 3 - H
 
-    def helpers(h, c, dst):
+    def helpers(h, c, dst, kind):
         base = h * 128 + c * 8
-        return [k for k in range(base, base + 8) if k not in group and k != dst and ct.may_write(k, dst)]
+        return [base + k for k in kind
+                if base + k not in group and base + k != dst and ct.may_write(base + k, dst)]
 
     def hc(core):
         return ct.host(core), ct.chip(core)
 
     out = []
-    if not ext:
+    if not got or (len(got) == 1 and got[0][0] == r):
         return [(None, None)]
-    leaves = [("z", e, j) for e, j in ext]
-    ec = [cores[e] for e, j in ext]
+    leaves = [("z", e, j) for e, j in got]
+    ec = [cores[e] for e, j in got]
     eh = [ct.host(c) for c in ec]
-    if len(ext) == 1:
+    if len(got) == 1:
         if eh[0] != D:
             return [(None, leaves[0])]
-        for R in helpers(C, ct.chip(rc), rc):
+        for R in helpers(C, ct.chip(rc), rc, OUTBOUND):
             out.append(("C", ("n", R, (leaves[0],))))
-        for R in helpers(P, ct.chip(ec[0]), rc):
+        for R in helpers(P, ct.chip(ec[0]), rc, INBOUND):
             out.append(("P", ("n", R, (leaves[0],))))
         return out
     nD = eh.count(D)
     if nD == 0:
-        if eh[0] == eh[1]:
+        kind = EITHER
+        if rc in ec:
+            chips = [hc(rc)]
+            if C in eh:
+                kind = INBOUND
+        elif eh[0] == eh[1]:
             chips = [hc(ec[0]), hc(ec[1])] + ([hc(rc)] if eh[0] == H else [])
+            if eh[0] == C:
+                kind = OUTBOUND
         elif H in eh:
             chips = [hc(ec[eh.index(H)]), hc(rc)]
+            if C in eh:
+                kind = INBOUND
         else:
             chips = [hc(rc)]
+            kind = INBOUND
         for h, c in chips:
-            for F in helpers(h, c, rc):
+            for F in helpers(h, c, rc, kind):
                 out.append((None, ("n", F, tuple(leaves))))
         return out
     if nD == 1:
@@ -102,23 +119,23 @@ def candidates(r, ext, cores, group):
         o = 1 - i
         if eh[o] != H:
             h, c = hc(ec[o])
-            for F in helpers(h, c, rc):
+            for F in helpers(h, c, rc, INBOUND if eh[o] == P else OUTBOUND):
                 out.append((None, ("n", F, tuple(leaves))))
             return out
-        for h, c in (hc(ec[o]), hc(rc)):
-            for F in helpers(h, c, rc):
-                for R in helpers(C, c, F):
+        for h, c in sorted(set((hc(ec[o]), hc(rc)))):
+            for F in helpers(h, c, rc, INBOUND):
+                for R in helpers(C, c, F, OUTBOUND):
                     out.append(("C", ("n", F, (leaves[o], ("n", R, (leaves[i],))))))
-                for R in helpers(P, ct.chip(ec[i]), F):
+                for R in helpers(P, ct.chip(ec[i]), F, INBOUND):
                     out.append(("P", ("n", F, (leaves[o], ("n", R, (leaves[i],))))))
         return out
     for i in (0, 1):
         h, c = hc(ec[i])
-        for R in helpers(C, ct.chip(rc), rc):
-            for F in helpers(h, c, R):
+        for R in helpers(C, ct.chip(rc), rc, OUTBOUND):
+            for F in helpers(h, c, R, OUTBOUND):
                 out.append(("C", ("n", R, (("n", F, tuple(leaves)),))))
-        for R in helpers(P, c, rc):
-            for F in helpers(h, c, R):
+        for R in helpers(P, c, rc, INBOUND):
+            for F in helpers(h, c, R, OUTBOUND):
                 out.append(("P", ("n", R, (("n", F, tuple(leaves)),))))
     return out
 
@@ -167,10 +184,10 @@ def split_flexible(cand, cores):
                 relay[H ^ 1] += flex[H] - x[H]
             mi = max(hin[h] + relay[h] for h in range(4))
             mo = max(hout[h] + relay[h] for h in range(4))
-            key = (max(mi, mo), mi + mo, x)
+            key = (max(mi, mo), mi + mo, sum(abs(2 * x[H] - flex[H]) for H in range(4)), x)
             if best is None or key < best:
                 best = key
-    return best[2]
+    return best[3]
 
 
 def choose_routes(route, cap, cores):
@@ -179,16 +196,15 @@ def choose_routes(route, cap, cores):
     lcache = {}
     cand = {}
     for (r, t), got in res.items():
-        ext = [(e, j) for e, j in got if e != r]
         cl = []
-        for via, tree in candidates(r, ext, cores, group):
+        for via, tree in candidates(r, got, cores, group):
             acc = []
             if tree is not None:
                 tree_writes(tree, cores[r], cores, acc)
             rs = []
             for sd in acc:
                 if sd not in lcache:
-                    lcache[sd] = links(sd[0], sd[1])
+                    lcache[sd] = links(sd[0], sd[1], group)
                 rs += lcache[sd]
             cl.append((via, tree, rs))
         cand[(r, t)] = cl
@@ -221,12 +237,21 @@ def choose_routes(route, cap, cores):
         return bi, bd
 
     choice, way = {}, {}
+
+    def lift(k):
+        rs = cand[k][choice[k]][2]
+        add(rs, -1)
+        return delta(rs)
+
+    def place(k, i):
+        choice[k] = i
+        add(cand[k][i][2], 1)
+
     keys = sorted(cand)
     for k in keys:
         if cand[k][0][0] is None:
             way[k] = None
-            choice[k] = best(k, None)[0]
-            add(cand[k][choice[k]][2], 1)
+            place(k, best(k, None)[0])
     for H in range(4):
         diffs = sorted((best(k, "C")[1] - best(k, "P")[1], k)
                        for k in keys if cand[k][0][0] is not None and ct.host(cores[k[0]]) == H)
@@ -234,15 +259,67 @@ def choose_routes(route, cap, cores):
             way[diffs[n][1]] = "C" if n < quota[H] else "P"
     for k in keys:
         if way[k] is not None:
-            choice[k] = best(k, way[k])[0]
-            add(cand[k][choice[k]][2], 1)
+            place(k, best(k, way[k])[0])
+    other = {"C": "P", "P": "C"}
     for p in range(PASSES):
         for k in keys:
             if len(cand[k]) > 1:
-                add(cand[k][choice[k]][2], -1)
-                choice[k] = best(k, way[k])[0]
-                add(cand[k][choice[k]][2], 1)
+                lift(k)
+                place(k, best(k, way[k])[0])
+        for H in range(4):
+            gain = {"C": [], "P": []}
+            for k in keys:
+                if way[k] is not None and ct.host(cores[k[0]]) == H:
+                    i = choice[k]
+                    freed = lift(k)
+                    gain[way[k]].append((freed - best(k, other[way[k]])[1], k))
+                    place(k, i)
+            gain["C"].sort(reverse=True)
+            gain["P"].sort(reverse=True)
+            for (ga, a), (gb, b) in zip(gain["C"], gain["P"]):
+                if ga + gb <= 0:
+                    break
+                ia, ib = choice[a], choice[b]
+                freed = lift(a) + lift(b)
+                na, da = best(a, "P")
+                place(a, na)
+                nb, db = best(b, "C")
+                place(b, nb)
+                if da + db < freed:
+                    way[a], way[b] = "P", "C"
+                else:
+                    lift(a)
+                    lift(b)
+                    place(a, ia)
+                    place(b, ib)
     return res, fill, {k: cand[k][choice[k]][1] for k in keys}
+
+
+def strides(tokens):
+    def rec(rem, k):
+        if not rem:
+            return []
+        if k == 0:
+            return None
+        a = min(rem)
+        opts = []
+        for s in range(1, 64):
+            n = 1
+            while a + n * s in rem:
+                n += 1
+                opts.append((n, -s))
+        opts.sort(reverse=True)
+        opts.append((1, -1))
+        for n, s in opts:
+            rest = rec(rem - frozenset(a - i * s for i in range(n)), k - 1)
+            if rest is not None:
+                return [(a, -s, n)] + rest
+        return None
+
+    for k in range(len(tokens) + 1):
+        got = rec(frozenset(tokens), k)
+        if got is not None:
+            return got
 
 
 def build_plan(route, cap, cores):
@@ -271,17 +348,15 @@ def build_plan(route, cap, cores):
         emit(me, phase, slots, dst, buf, slot, "fin" if final else "s%d" % (phase + 1))
         return phase
 
+    own, landed = {}, {}
     for (r, t) in sorted(trees):
         if trees[(r, t)] is not None:
             walk(trees[(r, t)], cores[r], "land", t, True)
-    own, landed = {}, {}
-    for (r, t), got in sorted(res.items()):
-        for e, j in got:
-            if e == r:
-                own.setdefault(r, []).append((t, j))
-        if trees[(r, t)] is not None:
             landed.setdefault(r, []).append(t)
-    return {"sends": sends, "expect": expect, "fill": fill, "own": own, "landed": landed}
+        elif res[(r, t)]:
+            own.setdefault(r, []).append((t, res[(r, t)][0][1]))
+    return {"sends": sends, "expect": expect, "fill": fill, "own": own,
+            "landed": {r: strides(ts) for r, ts in landed.items()}}
 
 
 def issue(g, core, T, batch):
@@ -313,16 +388,6 @@ def issue(g, core, T, batch):
     return len(batch)
 
 
-def runs_of(tokens):
-    out = []
-    for t in tokens:
-        if out and out[-1][1] == t:
-            out[-1][1] = t + 1
-        else:
-            out.append([t, t + 1])
-    return out
-
-
 def rank_program(g, core, T, topo):
     if "plan" not in CACHE:
         CACHE["plan"] = build_plan(T.tables["ROUTE"], T.tables["CAP"], list(T.cores))
@@ -351,11 +416,11 @@ def rank_program(g, core, T, topo):
     for t, j in plan["own"].get(rank, []):
         g.dma_start(T.y[t:t + 1], T.z[j:j + 1], accum_op=AluOpType.add).then_inc(T.sem.stored, 16)
         stored += 16
-    g.wait_ge(T.sem.stored, stored)
     if expect.get("fin", 0):
         g.wait_ge(T.sem.fin, expect["fin"])
-    for a, b in runs_of(plan["landed"].get(rank, [])):
-        g.dma_start(T.y[a:b], T.land[a:b], accum_op=AluOpType.add, max_dma_last_dim=4096).then_inc(T.sem.stored, 16)
+    for a, s, k in plan["landed"].get(rank, []):
+        b = a + (k - 1) * s + 1
+        g.dma_start(T.y[a:b:s], T.land[a:b:s], accum_op=AluOpType.add, max_dma_last_dim=4096).then_inc(T.sem.stored, 16)
         stored += 16
     g.wait_ge(T.sem.stored, stored)
     if sent:

from concourse.bass import DstId, RemoteDMATransfer
from concourse.mybir import AluOpType
import comms_topo as ct

SCRATCH = {
    "rows": ("dram", [48, 128, 8], "float32"),
    "land": ("dram", [24, 128, 8], "float32"),
}
SEMAPHORES = ["loaded", "read", "s1", "s2", "fin", "stored"]

CACHE = {}

OUTBOUND = (1, 5, 7)
INBOUND = (0, 3, 4, 6)
EITHER = (0, 1, 3, 4, 5, 6, 7)

SCALE = {"co": 48, "ci": 24, "po": 48, "pi": 48, "mate": 12, "so": 20, "si": 20, "cable": 4, "off": 32}
POWER = 12
PASSES = 6


def kept_results(route, cap):
    n = len(route)
    fill = [0] * n
    res = {}
    for r in range(n):
        for t in range(len(route[r])):
            got = []
            for e in route[r][t]:
                if fill[e] < cap:
                    got.append((e, fill[e]))
                    fill[e] += 1
            res[(r, t)] = got
    return res, fill


def links(src, dst, group):
    out = [("co", src), ("ci", dst)]
    hs, hd = ct.host(src), ct.host(dst)
    cs, cd = ct.chip(src), ct.chip(dst)
    if (hs, cs) == (hd, cd):
        return out
    out += [("po", hs, cs), ("pi", hd, cd)]
    if src in group:
        out.append(("off", src))
    die = (src % 8) // 4
    if ct.rack(hs) == ct.rack(hd):
        c = cs
        if (cs ^ cd) & 1:
            out.append(("mate", hs, cs, die))
            c = cs ^ 1
        if (hs, c) != (hd, cd):
            out += [("so", hs, c, die), ("si", hd, cd, die)]
    elif cs == cd:
        out.append(("cable", hs, cs, (src % 8) // 2))
    return out


def tree_writes(node, parent, cores, acc):
    if node[0] == "z":
        acc.append((cores[node[1]], parent))
    else:
        acc.append((node[1], parent))
        for ch in node[2]:
            tree_writes(ch, node[1], cores, acc)


def candidates(r, got, cores, group):
    rc = cores[r]
    H = ct.host(rc)
    D, P, C = H ^ 2, H ^ 1, 3 - H

    def helpers(h, c, dst, kind):
        base = h * 128 + c * 8
        return [base + k for k in kind
                if base + k not in group and base + k != dst and ct.may_write(base + k, dst)]

    def hc(core):
        return ct.host(core), ct.chip(core)

    out = []
    if not got or (len(got) == 1 and got[0][0] == r):
        return [(None, None)]
    leaves = [("z", e, j) for e, j in got]
    ec = [cores[e] for e, j in got]
    eh = [ct.host(c) for c in ec]
    if len(got) == 1:
        if eh[0] != D:
            return [(None, leaves[0])]
        for R in helpers(C, ct.chip(rc), rc, OUTBOUND):
            out.append(("C", ("n", R, (leaves[0],))))
        for R in helpers(P, ct.chip(ec[0]), rc, INBOUND):
            out.append(("P", ("n", R, (leaves[0],))))
        return out
    nD = eh.count(D)
    if nD == 0:
        kind = EITHER
        if rc in ec:
            chips = [hc(rc)]
            if C in eh:
                kind = INBOUND
        elif eh[0] == eh[1]:
            chips = [hc(ec[0]), hc(ec[1])] + ([hc(rc)] if eh[0] == H else [])
            if eh[0] == C:
                kind = OUTBOUND
        elif H in eh:
            chips = [hc(ec[eh.index(H)]), hc(rc)]
            if C in eh:
                kind = INBOUND
        else:
            chips = [hc(rc)]
            kind = INBOUND
        for h, c in chips:
            for F in helpers(h, c, rc, kind):
                out.append((None, ("n", F, tuple(leaves))))
        return out
    if nD == 1:
        i = eh.index(D)
        o = 1 - i
        if eh[o] != H:
            h, c = hc(ec[o])
            for F in helpers(h, c, rc, INBOUND if eh[o] == P else OUTBOUND):
                out.append((None, ("n", F, tuple(leaves))))
            return out
        for h, c in sorted(set((hc(ec[o]), hc(rc)))):
            for F in helpers(h, c, rc, INBOUND):
                for R in helpers(C, c, F, OUTBOUND):
                    out.append(("C", ("n", F, (leaves[o], ("n", R, (leaves[i],))))))
                for R in helpers(P, ct.chip(ec[i]), F, INBOUND):
                    out.append(("P", ("n", F, (leaves[o], ("n", R, (leaves[i],))))))
        return out
    for i in (0, 1):
        h, c = hc(ec[i])
        for R in helpers(C, ct.chip(rc), rc, OUTBOUND):
            for F in helpers(h, c, R, OUTBOUND):
                out.append(("C", ("n", R, (("n", F, tuple(leaves)),))))
        for R in helpers(P, c, rc, INBOUND):
            for F in helpers(h, c, R, OUTBOUND):
                out.append(("P", ("n", R, (("n", F, tuple(leaves)),))))
    return out


def split_flexible(cand, cores):
    hin, hout = [0] * 4, [0] * 4
    pair = {}
    flex = [0] * 4
    for (r, t), cl in cand.items():
        via, tree = cl[0][0], cl[0][1]
        H = ct.host(cores[r])
        if tree is None:
            continue
        if via is not None:
            flex[H] += 1
            hout[H ^ 2] += 1
            hin[H] += 1
            continue
        acc = []
        tree_writes(tree, cores[r], cores, acc)
        for s, d in acc:
            hs, hd = ct.host(s), ct.host(d)
            if hs != hd:
                hout[hs] += 1
                hin[hd] += 1
                if ct.rack(hs) != ct.rack(hd):
                    pair[(hs, hd)] = pair.get((hs, hd), 0) + 1
    per_rack = []
    for a in (0, 2):
        b = a + 1
        opts = []
        for xa in range(flex[a] + 1):
            for xb in range(flex[b] + 1):
                pa = pair.get((3 - a, a), 0) + xa + flex[b] - xb
                pb = pair.get((3 - b, b), 0) + xb + flex[a] - xa
                opts.append((max(pa, pb), xa, xb))
        least = min(opts)[0]
        per_rack.append([(xa, xb) for m, xa, xb in opts if m == least])
    best = None
    for x0, x1 in per_rack[0]:
        for x2, x3 in per_rack[1]:
            x = (x0, x1, x2, x3)
            relay = [0] * 4
            for H in range(4):
                relay[3 - H] += x[H]
                relay[H ^ 1] += flex[H] - x[H]
            mi = max(hin[h] + relay[h] for h in range(4))
            mo = max(hout[h] + relay[h] for h in range(4))
            key = (max(mi, mo), mi + mo, sum(abs(2 * x[H] - flex[H]) for H in range(4)), x)
            if best is None or key < best:
                best = key
    return best[3]


def choose_routes(route, cap, cores):
    group = set(cores)
    res, fill = kept_results(route, cap)
    lcache = {}
    cand = {}
    for (r, t), got in res.items():
        cl = []
        for via, tree in candidates(r, got, cores, group):
            acc = []
            if tree is not None:
                tree_writes(tree, cores[r], cores, acc)
            rs = []
            for sd in acc:
                if sd not in lcache:
                    lcache[sd] = links(sd[0], sd[1], group)
                rs += lcache[sd]
            cl.append((via, tree, rs))
        cand[(r, t)] = cl
    quota = split_flexible(cand, cores)
    tab = {c: [(i / s) ** POWER for i in range(600)] for c, s in SCALE.items()}
    load = {}

    def delta(rs):
        d = 0.0
        seen = {}
        for k in rs:
            n = load.get(k, 0) + seen.get(k, 0)
            tb = tab[k[0]]
            d += tb[n + 1] - tb[n]
            seen[k] = seen.get(k, 0) + 1
        return d

    def add(rs, s):
        for k in rs:
            load[k] = load.get(k, 0) + s

    def best(key, via):
        cl = cand[key]
        bi, bd = None, None
        for i in range(len(cl)):
            if cl[i][0] == via:
                d = delta(cl[i][2])
                if bd is None or d < bd:
                    bi, bd = i, d
        return bi, bd

    choice, way = {}, {}

    def lift(k):
        rs = cand[k][choice[k]][2]
        add(rs, -1)
        return delta(rs)

    def place(k, i):
        choice[k] = i
        add(cand[k][i][2], 1)

    keys = sorted(cand)
    for k in keys:
        if cand[k][0][0] is None:
            way[k] = None
            place(k, best(k, None)[0])
    for H in range(4):
        diffs = sorted((best(k, "C")[1] - best(k, "P")[1], k)
                       for k in keys if cand[k][0][0] is not None and ct.host(cores[k[0]]) == H)
        for n in range(len(diffs)):
            way[diffs[n][1]] = "C" if n < quota[H] else "P"
    for k in keys:
        if way[k] is not None:
            place(k, best(k, way[k])[0])
    other = {"C": "P", "P": "C"}
    for p in range(PASSES):
        for k in keys:
            if len(cand[k]) > 1:
                lift(k)
                place(k, best(k, way[k])[0])
        for H in range(4):
            gain = {"C": [], "P": []}
            for k in keys:
                if way[k] is not None and ct.host(cores[k[0]]) == H:
                    i = choice[k]
                    freed = lift(k)
                    gain[way[k]].append((freed - best(k, other[way[k]])[1], k))
                    place(k, i)
            gain["C"].sort(reverse=True)
            gain["P"].sort(reverse=True)
            for (ga, a), (gb, b) in zip(gain["C"], gain["P"]):
                if ga + gb <= 0:
                    break
                ia, ib = choice[a], choice[b]
                freed = lift(a) + lift(b)
                na, da = best(a, "P")
                place(a, na)
                nb, db = best(b, "C")
                place(b, nb)
                if da + db < freed:
                    way[a], way[b] = "P", "C"
                else:
                    lift(a)
                    lift(b)
                    place(a, ia)
                    place(b, ib)
    return res, fill, {k: cand[k][choice[k]][1] for k in keys}


def strides(tokens):
    def rec(rem, k):
        if not rem:
            return []
        if k == 0:
            return None
        a = min(rem)
        opts = []
        for s in range(1, 64):
            n = 1
            while a + n * s in rem:
                n += 1
                opts.append((n, -s))
        opts.sort(reverse=True)
        opts.append((1, -1))
        for n, s in opts:
            rest = rec(rem - frozenset(a - i * s for i in range(n)), k - 1)
            if rest is not None:
                return [(a, -s, n)] + rest
        return None

    for k in range(len(tokens) + 1):
        got = rec(frozenset(tokens), k)
        if got is not None:
            return got


def build_plan(route, cap, cores):
    res, fill, trees = choose_routes(route, cap, cores)
    sends = {}
    expect = {}
    used = {}

    def emit(core, phase, srcs, dst, buf, slot, sem):
        sends.setdefault(core, {}).setdefault(phase, []).append((srcs, dst, buf, slot, sem))
        ex = expect.setdefault(dst, {})
        ex[sem] = ex.get(sem, 0) + 1

    def walk(node, dst, buf, slot, final):
        if node[0] == "z":
            emit(cores[node[1]], 0, [node[2]], dst, buf, slot, "fin" if final else "s1")
            return 0
        me = node[1]
        slots, phase = [], 0
        for ch in node[2]:
            s = used.get(me, 0)
            used[me] = s + 1
            slots.append(s)
            phase = max(phase, walk(ch, me, "rows", s, False))
        phase += 1
        emit(me, phase, slots, dst, buf, slot, "fin" if final else "s%d" % (phase + 1))
        return phase

    own, landed = {}, {}
    for (r, t) in sorted(trees):
        if trees[(r, t)] is not None:
            walk(trees[(r, t)], cores[r], "land", t, True)
            landed.setdefault(r, []).append(t)
        elif res[(r, t)]:
            own.setdefault(r, []).append((t, res[(r, t)][0][1]))
    return {"sends": sends, "expect": expect, "fill": fill, "own": own,
            "landed": {r: strides(ts) for r, ts in landed.items()}}


def issue(g, core, T, batch):
    sem = {"s1": T.sem.s1, "s2": T.sem.s2, "fin": T.sem.fin}
    buf = {"rows": T.rows, "land": T.land}
    far = [s for s in batch if ct.mask(core, s[1]) != 0xFFFF]
    near = [s for s in batch if ct.mask(core, s[1]) == 0xFFFF]
    while far or near:
        bits = list(range(16))
        now = []
        for s in far[:8]:
            now.append((s, bits.pop(0)))
        far = far[8:]
        take = near[:len(bits)]
        near = near[len(bits):]
        for s in take:
            now.append((s, bits.pop()))
        transfers = []
        for (srcs, dst, b, slot, sm), bit in now:
            rid, pid = ct.addr(dst, core)
            if len(srcs) == 1:
                transfers.append(RemoteDMATransfer(dst_ids=[DstId(rid=rid, pnc=pid)], dma_engine_mask=1 << bit,
                                                   remote_sem=sem[sm], src=T.rows[srcs[0]], dst=buf[b][slot]))
            else:
                transfers.append(RemoteDMATransfer(dst_ids=[DstId(rid=rid, pnc=pid)], dma_engine_mask=1 << bit,
                                                   remote_sem=sem[sm], srcs=[T.rows[s] for s in srcs],
                                                   dsts=[buf[b][slot]], alu_op=1))
        g.remote_dma_fused(transfers, local_sem=T.sem.read)
    return len(batch)


def rank_program(g, core, T, topo):
    if "plan" not in CACHE:
        CACHE["plan"] = build_plan(T.tables["ROUTE"], T.tables["CAP"], list(T.cores))
    plan = CACHE["plan"]
    sends = plan["sends"].get(core, {})
    expect = plan["expect"].get(core, {})
    rank = T.rank_of(core)
    if rank is None:
        sent = 0
        for phase, sm in ((1, T.sem.s1), (2, T.sem.s2)):
            n = expect.get("s%d" % phase, 0)
            if n:
                g.wait_ge(sm, n)
            if sends.get(phase):
                sent += issue(g, core, T, sends[phase])
        if sent:
            g.wait_ge(T.sem.read, sent)
        return
    n = plan["fill"][rank]
    stored = 16
    g.dma_start(T.rows[0:n], T.z[0:n]).then_inc(T.sem.loaded, 16)
    g.dma_start(T.y[:], T.x[:]).then_inc(T.sem.stored, 16)
    g.wait_ge(T.sem.loaded, 16)
    sent = issue(g, core, T, sends.get(0, []))
    g.wait_ge(T.sem.stored, stored)
    for t, j in plan["own"].get(rank, []):
        g.dma_start(T.y[t:t + 1], T.z[j:j + 1], accum_op=AluOpType.add).then_inc(T.sem.stored, 16)
        stored += 16
    if expect.get("fin", 0):
        g.wait_ge(T.sem.fin, expect["fin"])
    for a, s, k in plan["landed"].get(rank, []):
        b = a + (k - 1) * s + 1
        g.dma_start(T.y[a:b:s], T.land[a:b:s], accum_op=AluOpType.add, max_dma_last_dim=4096).then_inc(T.sem.stored, 16)
        stored += 16
    g.wait_ge(T.sem.stored, stored)
    if sent:
        g.wait_ge(T.sem.read, sent)
